import numpy as np
import ml_dtypes


def mxq(x, axis, fmt="e4m3"):
    dtype, down = {"e4m3": (ml_dtypes.float8_e4m3fn, 7), "e5m2": (ml_dtypes.float8_e5m2, 14)}[fmt]
    v = np.moveaxis(np.asarray(x, np.float32).astype(ml_dtypes.bfloat16).astype(np.float64), axis, -1)
    blocks = v.reshape(v.shape[:-1] + (-1, 32))
    amax = np.abs(blocks).max(-1, keepdims=True)
    byte = np.maximum(np.where(amax > 0, np.frexp(amax)[1] - 1 + 127, 0) - down, 1)
    scale = np.exp2(byte - 127.0)
    codes = (blocks / scale).astype(np.float32).astype(dtype).astype(np.float64)
    return np.moveaxis((codes * scale).reshape(v.shape), -1, axis)


WIDE = False


def mx_kscale(k):
    if not WIDE:
        return np.ones(k)
    levels = np.array([30, -30])
    if k % 512:
        return np.exp2(np.random.permutation(np.resize(levels, k // 32))).repeat(32)
    a = np.empty((k // 512, 16))
    for p in range(k // 512):
        a[p, :8] = np.random.permutation(np.resize(levels, 8))
        for g in range(8):
            far = levels[np.abs(levels - a[p, g]) >= 10]
            a[p, g + 8] = far[np.random.randint(len(far))]
    return np.exp2(a.ravel()).repeat(32)


def f64(x):
    return np.asarray(x).astype(np.float64)


def striped(idx):
    return np.tile(np.asarray(idx).reshape(-1, 16).T, (8, 1)).astype(np.uint16)


def unstriped(offs):
    return offs[:16].T.reshape(-1).astype(np.int64)


E2M1 = np.array([0.0, 0.5, 1.0, 1.5, 2.0, 3.0, 4.0, 6.0, -0.0, -0.5, -1.0, -1.5, -2.0, -3.0, -4.0, -6.0])


def pack_weight(w, fmt):
    k, n = w.shape
    w = f64(np.asarray(w, np.float32).astype(ml_dtypes.bfloat16)).reshape(k // 32, 32, n)
    amax = np.abs(w).max(1)
    if fmt == "e4m3":
        byte = np.frexp(amax)[1] - 1 + 127 - 7
    else:
        mant, ex = np.frexp(amax / 6.0)
        byte = np.where(mant > 0.5, ex, ex - 1) + 127
    byte = np.clip(np.where(amax > 0, byte, 1), 1, 254)
    scaled = (w * np.exp2(127.0 - byte)[:, None, :]).reshape(k, n).astype(np.float32)
    by_word = np.ascontiguousarray(scaled.reshape(k // 512, 128, 4, n).transpose(0, 1, 3, 2))
    if fmt == "e4m3":
        words = by_word.astype(ml_dtypes.float8_e4m3fn).view(np.uint8)
    else:
        c = by_word.astype(ml_dtypes.float4_e2m1fn).view(np.uint8) & 0xF
        words = (c[..., 0::2] | (c[..., 1::2] << 4)).reshape(k // 512, 128, 2 * n)
    return np.ascontiguousarray(words), np.ascontiguousarray(byte.astype(np.uint8).reshape(k // 512, 16, n))


def unpack_weight(words, scales, fmt):
    g, _, n = scales.shape
    words = np.ascontiguousarray(words).reshape(g, 128, n, -1)
    if fmt == "e4m3":
        vals = words.view(ml_dtypes.float8_e4m3fn).astype(np.float64)
    else:
        nib = np.empty((g, 128, n, 4), np.uint8)
        nib[..., 0::2] = words & 0xF
        nib[..., 1::2] = words >> 4
        vals = E2M1[nib]
    vals = vals * np.repeat(np.exp2(scales.astype(np.float64) - 127.0), 8, axis=1)[..., None]
    return vals.transpose(0, 1, 3, 2).reshape(g * 512, n)


K, T, J, S, R, F, Z, V, N = 512, 512, 256, 512, 512, 512, 1024, 512, 256


def setup_inputs():
    n = np.random.standard_normal
    idx = np.random.permutation(T)[:J]
    idx2 = np.random.permutation(S)[:J]
    idx3 = np.random.permutation(Z)[:J]
    idx4 = np.random.permutation(V)[:J]
    fk = mx_kscale(K)
    fr = mx_kscale(R)
    ff = mx_kscale(F)
    wp = pack_weight(n((K, R)) * 1 / np.sqrt(K) * fk[:, None] * fr, "e2m1")
    w2p = pack_weight(n((F, R)) * 1 / np.sqrt(F) * ff[:, None] * fr, "e2m1")
    wbp = pack_weight(n((R, N)) * 1 / np.sqrt(R) / fr[:, None], "e4m3")
    return {
        "xa": (n((K, T))).astype(np.float32),
        "xb": (n((K, S))).astype(np.float32),
        "hb": (np.random.uniform(0.2, 0.9, (K, 1))).astype(np.float32),
        "fk": (np.random.uniform(0.5, 2.0, (K, 1)) / fk[:, None]).astype(np.float32),
        "w_words": wp[0],
        "w_scales": wp[1],
        "xo": (n((F, Z))).astype(np.float32),
        "fl": (np.random.uniform(0.5, 2.0, (F, 1)) / ff[:, None]).astype(np.float32),
        "so": (n((F, J)) * 0.8).astype(np.float32),
        "w2_words": w2p[0],
        "w2_scales": w2p[1],
        "tb": (n((R, V)) * 0.7 * fr[:, None]).astype(np.float32),
        "wb_words": wbp[0],
        "wb_scales": wbp[1],
        "rs": (n((N, J))).astype(np.float32),
        "gm": (np.random.uniform(0.5, 2.0, (N, 1))).astype(np.float32),
        "offs": striped(idx),
        "offs2": striped(idx2),
        "offs3": striped(idx3),
        "offs4": striped(idx4),
    }


def reference(xa, xb, hb, fk, w_words, w_scales, xo, fl, so, w2_words, w2_scales, tb, wb_words, wb_scales, rs, gm, offs, offs2, offs3, offs4):
    idx = unstriped(offs)
    idx2 = unstriped(offs2)
    idx3 = unstriped(offs3)
    idx4 = unstriped(offs4)
    wu = unpack_weight(w_words, w_scales, "e2m1")
    w2u = unpack_weight(w2_words, w2_scales, "e2m1")
    wbu = unpack_weight(wb_words, wb_scales, "e4m3")
    u = (f64(xa)[:, idx] - np.minimum(f64(xb)[:, idx2], f64(hb))) * f64(fk)
    u2 = np.maximum(f64(xo)[:, idx3], f64(so)) * f64(fl)
    uq = mxq(u, 0, "e4m3")
    u2q = mxq(u2, 0, "e4m3")
    a = wu.T @ uq + w2u.T @ u2q
    hid = np.maximum(a, f64(tb)[:, idx4])
    hidq = mxq(hid, 0, "e5m2")
    p = wbu.T @ hidq
    y = f64(gm) * p + f64(rs)
    return y

@@ -1,0 +1,229 @@
+from contextlib import ExitStack
+
+import concourse.mybir as mybir
+
+K, T, J, S, R, F, Z, V, N = 512, 512, 256, 512, 512, 512, 1024, 512, 256
+FLOPS = 2 * J * (K * R + F * R + R * N)
+
+F32 = mybir.dt.float32
+BF16 = mybir.dt.bfloat16
+I32 = mybir.dt.int32
+U32 = mybir.dt.uint32
+U16 = mybir.dt.uint16
+U8 = mybir.dt.uint8
+E4M3 = mybir.dt.float8_e4m3fn_x4
+E5M2 = mybir.dt.float8_e5m2_x4
+E2M1 = mybir.dt.float4_e2m1fn_x4
+ALU = mybir.AluOpType
+COPY = mybir.ActivationFunctionType.Copy
+
+P = 128
+PACK = 4
+HALF = J // 2
+RUN = 4
+LIST_COLS = J // 16
+
+
+def tile_list_sum_boundedgaps_largest_abovetable_residual_kernel(
+    tc, xa, xb, hb, fk, w_words, w_scales, xo, fl, so, w2_words, w2_scales, tb,
+    wb_words, wb_scales, rs, gm, offs, offs2, offs3, offs4, out,
+):
+    nc = tc.nc
+    with ExitStack() as ctx:
+        pool = ctx.enter_context(tc.tile_pool(name="held", bufs=1))
+        psum = ctx.enter_context(tc.psum_pool(name="psum", bufs=1))
+
+        def sb(name, shape, dtype):
+            return pool.tile(shape, dtype, name=name, align_bytes=64)
+
+        list_a = sb("list_a", [P, LIST_COLS], U16)
+        list_b = sb("list_b", [P, LIST_COLS], U16)
+        list_o = sb("list_o", [P, LIST_COLS], U16)
+        list_t = sb("list_t", [P, LIST_COLS], U16)
+        xa_sb = [sb(f"xa{g}", [P, 2 * T], F32) for g in range(2)]
+        xb_sb = [sb(f"xb{g}", [P, 2 * S], F32) for g in range(2)]
+        xo_sb = [sb(f"xo{t}", [P, Z], F32) for t in range(PACK)]
+        tb_sb = [sb(f"tb{t}", [P, V], F32) for t in range(PACK)]
+        so_sb = sb("so_sb", [P, PACK, J], F32)
+        rs_sb = sb("rs_sb", [P, 2, J], F32)
+        hb_sb = sb("hb_sb", [P, PACK], F32)
+        fk_sb = sb("fk_sb", [P, PACK], F32)
+        fl_sb = sb("fl_sb", [P, PACK], F32)
+        gm_sb = sb("gm_sb", [P, 2], F32)
+        words_in = sb("words_in", [P, 4 * R], U8)
+        scales_in = sb("scales_in", [P, 2 * R + N], U8)
+        wb_codes = sb("wb_codes", [P, N], U32)
+
+        def plane(x, t):
+            return x.rearrange("(p t) c -> p t c", t=PACK)[:, t, :]
+
+        def load(dst, src):
+            nc.sync.dma_start(dst, src)
+
+        def load_scale_rows(src, col0, q, queue=nc.sync):
+            width = src.shape[2]
+            queue.dma_start(
+                scales_in[32 * q : 32 * q + 4, col0 : col0 + width].bitcast(I32),
+                src[0, 4 * q : 4 * q + 4, :].bitcast(I32),
+            )
+
+        def by_partition(vec):
+            return vec.rearrange("(p t) o -> p (t o)", t=PACK)
+
+        nc.vector.memset(scales_in[:].bitcast(I32), 0)
+
+        xa_pairs = xa.rearrange("(p g e) c -> p g (e c)", g=2, e=2)
+        xb_pairs = xb.rearrange("(p g e) c -> p g (e c)", g=2, e=2)
+        load(xb_sb[0][:], xb_pairs[:, 0, :])
+        load(list_b[:], offs2)
+        load(xa_sb[0][:], xa_pairs[:, 0, :])
+        load(list_a[:], offs)
+        load(fk_sb[:], by_partition(fk))
+        load(hb_sb[:], by_partition(hb))
+        load(xb_sb[1][:], xb_pairs[:, 1, :])
+        load(xa_sb[1][:], xa_pairs[:, 1, :])
+        for q in range(4):
+            load_scale_rows(w2_scales, R, q, nc.gpsimd)
+        load(list_o[:], offs3)
+        load_scale_rows(w_scales, 0, 0)
+        load(xo_sb[0][:], plane(xo, 0))
+        load_scale_rows(w_scales, 0, 1)
+        load_scale_rows(w_scales, 0, 2)
+        load(xo_sb[1][:], plane(xo, 1))
+        load_scale_rows(w_scales, 0, 3)
+        load(words_in[:, 0 : 2 * R].bitcast(I32), w_words[0].bitcast(I32))
+        load(words_in[:, 2 * R : 4 * R].bitcast(I32), w2_words[0].bitcast(I32))
+        load(so_sb[:, 0:3, :], so.rearrange("(p t) c -> p t c", t=PACK)[:, 0:3, :])
+        load(fl_sb[:], by_partition(fl))
+        load(xo_sb[2][:], plane(xo, 2))
+        load(list_t[:], offs4)
+        load(xo_sb[3][:], plane(xo, 3))
+        load(so_sb[:, 3, :], plane(so, 3))
+        for t in range(PACK):
+            load(tb_sb[t][:], plane(tb, t))
+        load(wb_codes[:].bitcast(I32), wb_words[0].rearrange("p n t -> p (n t)").bitcast(I32))
+        load(rs_sb[:], rs.rearrange("(h p) c -> p h c", h=2))
+        for q in range(4):
+            load_scale_rows(wb_scales, 2 * R, q)
+        with nc.allow_non_contiguous_dma(reason="one factor for each output row"):
+            load(gm_sb[:], gm.rearrange("(h p) o -> p (h o)", h=2))
+
+        def woven(x):
+            return x.rearrange("p (c i t) -> p c t i", i=RUN, t=PACK)
+
+        def in_runs(x):
+            return x.rearrange("p t (c i) -> p c t i", i=RUN)
+
+        def spread(vec, width):
+            return vec[:].unsqueeze(1).unsqueeze(3).to_broadcast([P, width // RUN, PACK, RUN])
+
+        def half_cols(h):
+            return slice(h * HALF, (h + 1) * HALF)
+
+        def half_list(lst, h):
+            return lst[:, h * LIST_COLS // 2 : (h + 1) * LIST_COLS // 2]
+
+        fk_neg = sb("fk_neg", [P, PACK], F32)
+        nc.scalar.activation(fk_neg[:], fk_sb[:], COPY, scale=-1.0)
+        ga = sb("ga", [P, PACK, J], F32)
+        gb = sb("gb", [P, PACK, J], F32)
+        gap = sb("gap", [P, PACK, J], F32)
+        for t in range(PACK):
+            cols = slice((t % 2) * S, (t % 2 + 1) * S)
+            nc.scalar.activation(gb[:, t, :], xb_sb[t // 2][:, cols].indirect(list_b[:]), COPY)
+            nc.vector.tensor_copy(ga[:, t, :], xa_sb[t // 2][:, cols].indirect(list_a[:]))
+            nc.vector.scalar_tensor_tensor(
+                gap[:, t, :], gb[:, t, :], hb_sb[:, t : t + 1], ga[:, t, :], ALU.min, ALU.subtract
+            )
+        u_bf = sb("u_bf", [P, PACK * J], BF16)
+        nc.vector.tensor_tensor(woven(u_bf[:]), in_runs(gap[:]), spread(fk_neg, J), ALU.mult)
+        u_codes = sb("u_codes", [P, J], U32)
+        u_scales = sb("u_scales", [P, J], U8)
+        nc.vector.quantize_mx(u_codes[:].bitcast(E4M3), u_scales[:], u_bf[:])
+
+        words = sb("words", [P, 4 * R], U8)
+        scales = sb("scales", [P, 2 * R], U8)
+        nc.scalar.copy(
+            words[:].bitcast(U16).rearrange("p (w t m) -> p w t m", w=2, t=PACK),
+            words_in[:].bitcast(U16).rearrange("p (w m t) -> p w t m", w=2, t=PACK),
+        )
+        nc.vector.tensor_copy(
+            scales[:].rearrange("p (w t m) -> p w t m", w=2, t=PACK),
+            scales_in[:, 0 : 2 * R].rearrange("p (w m t) -> p w t m", w=2, t=PACK),
+        )
+
+        acc = [psum.tile([P, PACK, HALF], F32, name=f"acc{h}") for h in range(2)]
+
+        def first_stage(h, w, codes, planes):
+            for t in range(PACK):
+                col = w * R + t * P
+                nc.tensor.matmul_mx(
+                    acc[h][:, t, :],
+                    lhsT=words[:, 2 * col : 2 * (col + P)].bitcast(E2M1),
+                    lhsT_scale=scales[:, col : col + P],
+                    rhs=codes.bitcast(E4M3),
+                    rhs_scale=planes,
+                    start=(w == 0 and t == 0),
+                    stop=(w == 1 and t == PACK - 1),
+                )
+
+        for h in range(2):
+            first_stage(h, 0, u_codes[:, half_cols(h)], u_scales[:, half_cols(h)])
+
+        go = sb("go", [P, PACK, J], F32)
+        larger = sb("larger", [P, PACK, J], F32)
+        for t in range(PACK - 1):
+            nc.scalar.activation(go[:, t, :], xo_sb[t][:].indirect(list_o[:]), COPY)
+            nc.vector.tensor_tensor(larger[:, t, :], go[:, t, :], so_sb[:, t, :], ALU.max)
+        last = PACK - 1
+        nc.vector.tensor_copy(go[:, last, half_cols(0)], xo_sb[last][:].indirect(half_list(list_o, 0)))
+        nc.scalar.activation(go[:, last, half_cols(1)], xo_sb[last][:].indirect(half_list(list_o, 1)), COPY)
+        for h in range(2):
+            nc.vector.tensor_tensor(
+                larger[:, last, half_cols(h)], go[:, last, half_cols(h)], so_sb[:, last, half_cols(h)], ALU.max
+            )
+        u2_bf = [sb(f"u2_bf{h}", [P, PACK * HALF], BF16) for h in range(2)]
+        for h in range(2):
+            nc.vector.tensor_tensor(
+                woven(u2_bf[h][:]), in_runs(larger[:, :, half_cols(h)]), spread(fl_sb, HALF), ALU.mult
+            )
+        for h in range(2):
+            u2_codes = sb(f"u2_codes{h}", [P, HALF], U32)
+            u2_scales = sb(f"u2_scales{h}", [P, HALF], U8)
+            nc.vector.quantize_mx(u2_codes[:].bitcast(E4M3), u2_scales[:], u2_bf[h][:])
+            first_stage(h, 1, u2_codes[:], u2_scales[:])
+
+        gt = sb("gt", [P, PACK, J], F32)
+        for t in range(PACK - 1):
+            nc.scalar.activation(gt[:, t, :], tb_sb[t][:].indirect(list_t[:]), COPY)
+        for h in range(2):
+            nc.scalar.activation(gt[:, last, half_cols(h)], tb_sb[last][:].indirect(half_list(list_t, h)), COPY)
+
+        hid_bf = [sb(f"hid_bf{h}", [P, PACK * HALF], BF16) for h in range(2)]
+        for h in range(2):
+            nc.vector.tensor_tensor(
+                woven(hid_bf[h][:]), in_runs(acc[h][:]), in_runs(gt[:, :, half_cols(h)]), ALU.max
+            )
+        prod = [psum.tile([P, 2, HALF], F32, name=f"prod{h}") for h in range(2)]
+        for h in range(2):
+            hid_codes = sb(f"hid_codes{h}", [P, HALF], U32)
+            hid_scales = sb(f"hid_scales{h}", [P, HALF], U8)
+            nc.vector.quantize_mx(hid_codes[:].bitcast(E5M2), hid_scales[:], hid_bf[h][:])
+            for g in range(2):
+                nc.tensor.matmul_mx(
+                    prod[h][:, g, :],
+                    lhsT=wb_codes[:, g * P : (g + 1) * P].bitcast(E4M3),
+                    lhsT_scale=scales_in[:, 2 * R + g * P : 2 * R + (g + 1) * P],
+                    rhs=hid_codes[:].bitcast(E5M2),
+                    rhs_scale=hid_scales[:],
+                    start=True,
+                    stop=True,
+                )
+        out_rows = out.rearrange("(g p) c -> p g c", g=2)
+        for h in range(2):
+            y = sb(f"y{h}", [P, 2, HALF], F32)
+            for g in range(2):
+                nc.vector.scalar_tensor_tensor(
+                    y[:, g, :], prod[h][:, g, :], gm_sb[:, g : g + 1], rs_sb[:, g, half_cols(h)], ALU.mult, ALU.add
+                )
+            nc.sync.dma_start(out_rows[:, :, half_cols(h)], y[:])

@@ -42,20 +42,18 @@ def tile_list_sum_boundedgaps_largest_abovetable_residual_kernel(
         list_t = sb("list_t", [P, LIST_COLS], U16)
         xa_sb = [sb(f"xa{g}", [P, 2 * T], F32) for g in range(2)]
         xb_sb = [sb(f"xb{g}", [P, 2 * S], F32) for g in range(2)]
-        xo_sb = [sb(f"xo{t}", [P, Z], F32) for t in range(PACK)]
-        tb_sb = [sb(f"tb{t}", [P, V], F32) for t in range(PACK)]
+        xo_pair = sb("xo_pair", [P, 2 * Z], F32)
+        xo_sb = [xo_pair[:, 0:Z], xo_pair[:, Z : 2 * Z]] + [sb(f"xo{t}", [P, Z], F32)[:] for t in (2, 3)]
+        tb_sb = [sb(f"tb{t}", [P, V], F32)[:] for t in range(PACK)]
         so_sb = sb("so_sb", [P, PACK, J], F32)
         rs_sb = sb("rs_sb", [P, 2, J], F32)
         hb_sb = sb("hb_sb", [P, PACK], F32)
         fk_sb = sb("fk_sb", [P, PACK], F32)
         fl_sb = sb("fl_sb", [P, PACK], F32)
         gm_sb = sb("gm_sb", [P, 2], F32)
-        words_in = sb("words_in", [P, 4 * R], U8)
+        words_in = [sb(f"words_in{w}", [P, 2 * R], U8) for w in range(2)]
         scales_in = sb("scales_in", [P, 2 * R + N], U8)
         wb_codes = sb("wb_codes", [P, N], U32)
-
-        def plane(x, t):
-            return x.rearrange("(p t) c -> p t c", t=PACK)[:, t, :]
 
         def load(dst, src):
             nc.sync.dma_start(dst, src)
@@ -72,35 +70,33 @@ def tile_list_sum_boundedgaps_largest_abovetable_residual_kernel(
 
         nc.vector.memset(scales_in[:].bitcast(I32), 0)
 
-        xa_pairs = xa.rearrange("(p g e) c -> p g (e c)", g=2, e=2)
-        xb_pairs = xb.rearrange("(p g e) c -> p g (e c)", g=2, e=2)
-        load(xb_sb[0][:], xb_pairs[:, 0, :])
-        load(list_b[:], offs2)
-        load(xa_sb[0][:], xa_pairs[:, 0, :])
-        load(list_a[:], offs)
+        def planes(x, t0, t1):
+            return x.rearrange("(p t) c -> p (t c)", t=PACK)[:, t0 * x.shape[1] : t1 * x.shape[1]]
+
+        load(xb_sb[0][:], planes(xb, 0, 2))
         load(fk_sb[:], by_partition(fk))
+        load(list_b[:], offs2)
+        load(xa_sb[0][:], planes(xa, 0, 2))
+        load(list_a[:], offs)
         load(hb_sb[:], by_partition(hb))
-        load(xb_sb[1][:], xb_pairs[:, 1, :])
-        load(xa_sb[1][:], xa_pairs[:, 1, :])
+        load(xb_sb[1][:], planes(xb, 2, 4))
+        load(xa_sb[1][:], planes(xa, 2, 4))
         for q in range(4):
             load_scale_rows(w2_scales, R, q, nc.gpsimd)
         load(list_o[:], offs3)
-        load_scale_rows(w_scales, 0, 0)
-        load(xo_sb[0][:], plane(xo, 0))
-        load_scale_rows(w_scales, 0, 1)
-        load_scale_rows(w_scales, 0, 2)
-        load(xo_sb[1][:], plane(xo, 1))
-        load_scale_rows(w_scales, 0, 3)
-        load(words_in[:, 0 : 2 * R].bitcast(I32), w_words[0].bitcast(I32))
-        load(words_in[:, 2 * R : 4 * R].bitcast(I32), w2_words[0].bitcast(I32))
-        load(so_sb[:, 0:3, :], so.rearrange("(p t) c -> p t c", t=PACK)[:, 0:3, :])
+        load(xo_pair[:], planes(xo, 0, 2))
+        for q in range(4):
+            load_scale_rows(w_scales, 0, q)
+        load(so_sb[:, 0:2, :].rearrange("p t c -> p (t c)"), planes(so, 0, 2))
+        load(xo_sb[2], planes(xo, 2, 3))
+        load(words_in[0][:].bitcast(I32), w_words[0].bitcast(I32))
         load(fl_sb[:], by_partition(fl))
-        load(xo_sb[2][:], plane(xo, 2))
+        load(xo_sb[3], planes(xo, 3, 4))
+        load(so_sb[:, 2:4, :].rearrange("p t c -> p (t c)"), planes(so, 2, 4))
+        load(words_in[1][:].bitcast(I32), w2_words[0].bitcast(I32))
         load(list_t[:], offs4)
-        load(xo_sb[3][:], plane(xo, 3))
-        load(so_sb[:, 3, :], plane(so, 3))
         for t in range(PACK):
-            load(tb_sb[t][:], plane(tb, t))
+            load(tb_sb[t], planes(tb, t, t + 1))
         load(wb_codes[:].bitcast(I32), wb_words[0].rearrange("p n t -> p (n t)").bitcast(I32))
         load(rs_sb[:], rs.rearrange("(h p) c -> p h c", h=2))
         for q in range(4):
@@ -123,6 +119,12 @@ def tile_list_sum_boundedgaps_largest_abovetable_residual_kernel(
         def half_list(lst, h):
             return lst[:, h * LIST_COLS // 2 : (h + 1) * LIST_COLS // 2]
 
+        def gather(dst, window, lst, on_vector):
+            if on_vector:
+                nc.vector.tensor_copy(dst, window.indirect(lst))
+            else:
+                nc.scalar.activation(dst, window.indirect(lst), COPY)
+
         fk_neg = sb("fk_neg", [P, PACK], F32)
         nc.scalar.activation(fk_neg[:], fk_sb[:], COPY, scale=-1.0)
         ga = sb("ga", [P, PACK, J], F32)
@@ -130,8 +132,8 @@ def tile_list_sum_boundedgaps_largest_abovetable_residual_kernel(
         gap = sb("gap", [P, PACK, J], F32)
         for t in range(PACK):
             cols = slice((t % 2) * S, (t % 2 + 1) * S)
-            nc.scalar.activation(gb[:, t, :], xb_sb[t // 2][:, cols].indirect(list_b[:]), COPY)
-            nc.vector.tensor_copy(ga[:, t, :], xa_sb[t // 2][:, cols].indirect(list_a[:]))
+            gather(gb[:, t, :], xb_sb[t // 2][:, cols], list_b[:], False)
+            gather(ga[:, t, :], xa_sb[t // 2][:, cols], list_a[:], t < PACK - 1)
             nc.vector.scalar_tensor_tensor(
                 gap[:, t, :], gb[:, t, :], hb_sb[:, t : t + 1], ga[:, t, :], ALU.min, ALU.subtract
             )
@@ -141,28 +143,29 @@ def tile_list_sum_boundedgaps_largest_abovetable_residual_kernel(
         u_scales = sb("u_scales", [P, J], U8)
         nc.vector.quantize_mx(u_codes[:].bitcast(E4M3), u_scales[:], u_bf[:])
 
-        words = sb("words", [P, 4 * R], U8)
+        words = [sb(f"words{w}", [P, 2 * R], U8) for w in range(2)]
         scales = sb("scales", [P, 2 * R], U8)
-        nc.scalar.copy(
-            words[:].bitcast(U16).rearrange("p (w t m) -> p w t m", w=2, t=PACK),
-            words_in[:].bitcast(U16).rearrange("p (w m t) -> p w t m", w=2, t=PACK),
-        )
         nc.vector.tensor_copy(
             scales[:].rearrange("p (w t m) -> p w t m", w=2, t=PACK),
             scales_in[:, 0 : 2 * R].rearrange("p (w m t) -> p w t m", w=2, t=PACK),
         )
+        for w in range(2):
+            nc.scalar.copy(
+                words[w][:].bitcast(U16).rearrange("p (t m) -> p t m", t=PACK),
+                words_in[w][:].bitcast(U16).rearrange("p (m t) -> p t m", t=PACK),
+            )
 
         acc = [psum.tile([P, PACK, HALF], F32, name=f"acc{h}") for h in range(2)]
 
-        def first_stage(h, w, codes, planes):
+        def first_stage(h, w, codes, moving_scales):
             for t in range(PACK):
-                col = w * R + t * P
+                col = t * P
                 nc.tensor.matmul_mx(
                     acc[h][:, t, :],
-                    lhsT=words[:, 2 * col : 2 * (col + P)].bitcast(E2M1),
-                    lhsT_scale=scales[:, col : col + P],
+                    lhsT=words[w][:, 2 * col : 2 * (col + P)].bitcast(E2M1),
+                    lhsT_scale=scales[:, w * R + col : w * R + col + P],
                     rhs=codes.bitcast(E4M3),
-                    rhs_scale=planes,
+                    rhs_scale=moving_scales,
                     start=(w == 0 and t == 0),
                     stop=(w == 1 and t == PACK - 1),
                 )
@@ -173,14 +176,14 @@ def tile_list_sum_boundedgaps_largest_abovetable_residual_kernel(
         go = sb("go", [P, PACK, J], F32)
         larger = sb("larger", [P, PACK, J], F32)
         for t in range(PACK - 1):
-            nc.scalar.activation(go[:, t, :], xo_sb[t][:].indirect(list_o[:]), COPY)
-            nc.vector.tensor_tensor(larger[:, t, :], go[:, t, :], so_sb[:, t, :], ALU.max)
+            nc.scalar.activation(go[:, t, :], xo_sb[t].indirect(list_o[:]), COPY)
+        nc.vector.tensor_tensor(larger[:, 0:2, :], go[:, 0:2, :], so_sb[:, 0:2, :], ALU.max)
         last = PACK - 1
-        nc.vector.tensor_copy(go[:, last, half_cols(0)], xo_sb[last][:].indirect(half_list(list_o, 0)))
-        nc.scalar.activation(go[:, last, half_cols(1)], xo_sb[last][:].indirect(half_list(list_o, 1)), COPY)
+        nc.vector.tensor_copy(go[:, last, half_cols(0)], xo_sb[last].indirect(half_list(list_o, 0)))
+        nc.scalar.activation(go[:, last, half_cols(1)], xo_sb[last].indirect(half_list(list_o, 1)), COPY)
         for h in range(2):
             nc.vector.tensor_tensor(
-                larger[:, last, half_cols(h)], go[:, last, half_cols(h)], so_sb[:, last, half_cols(h)], ALU.max
+                larger[:, 2:4, half_cols(h)], go[:, 2:4, half_cols(h)], so_sb[:, 2:4, half_cols(h)], ALU.max
             )
         u2_bf = [sb(f"u2_bf{h}", [P, PACK * HALF], BF16) for h in range(2)]
         for h in range(2):
@@ -194,10 +197,11 @@ def tile_list_sum_boundedgaps_largest_abovetable_residual_kernel(
             first_stage(h, 1, u2_codes[:], u2_scales[:])
 
         gt = sb("gt", [P, PACK, J], F32)
-        for t in range(PACK - 1):
-            nc.scalar.activation(gt[:, t, :], tb_sb[t][:].indirect(list_t[:]), COPY)
-        for h in range(2):
-            nc.scalar.activation(gt[:, last, half_cols(h)], tb_sb[last][:].indirect(half_list(list_t, h)), COPY)
+        for t in range(2):
+            gather(gt[:, t, :], tb_sb[t], list_t[:], False)
+        for t in range(2, PACK):
+            for h in range(2):
+                gather(gt[:, t, half_cols(h)], tb_sb[t], half_list(list_t, h), h == 0)
 
         hid_bf = [sb(f"hid_bf{h}", [P, PACK * HALF], BF16) for h in range(2)]
         for h in range(2):
@@ -226,4 +230,4 @@ def tile_list_sum_boundedgaps_largest_abovetable_residual_kernel(
                 nc.vector.scalar_tensor_tensor(
                     y[:, g, :], prod[h][:, g, :], gm_sb[:, g : g + 1], rs_sb[:, g, half_cols(h)], ALU.mult, ALU.add
                 )
-            nc.sync.dma_start(out_rows[:, :, half_cols(h)], y[:])
+                nc.sync.dma_start(out_rows[:, g, half_cols(h)], y[:, g, :])

@@ -41,7 +41,7 @@ def tile_list_sum_boundedgaps_largest_abovetable_residual_kernel(
         list_o = sb("list_o", [P, LIST_COLS], U16)
         list_t = sb("list_t", [P, LIST_COLS], U16)
         xa_sb = [sb(f"xa{g}", [P, 2 * T], F32) for g in range(2)]
-        xb_sb = [sb(f"xb{g}", [P, 2 * S], F32) for g in range(2)]
+        xb_sb = sb("xb_sb", [P, PACK * S], F32)
         xo_pair = sb("xo_pair", [P, 2 * Z], F32)
         xo_sb = [xo_pair[:, 0:Z], xo_pair[:, Z : 2 * Z]] + [sb(f"xo{t}", [P, Z], F32)[:] for t in (2, 3)]
         tb_sb = [sb(f"tb{t}", [P, V], F32)[:] for t in range(PACK)]
@@ -73,13 +73,12 @@ def tile_list_sum_boundedgaps_largest_abovetable_residual_kernel(
         def planes(x, t0, t1):
             return x.rearrange("(p t) c -> p (t c)", t=PACK)[:, t0 * x.shape[1] : t1 * x.shape[1]]
 
-        load(xb_sb[0][:], planes(xb, 0, 2))
+        load(xb_sb[:], planes(xb, 0, 4))
         load(fk_sb[:], by_partition(fk))
         load(list_b[:], offs2)
         load(xa_sb[0][:], planes(xa, 0, 2))
         load(list_a[:], offs)
         load(hb_sb[:], by_partition(hb))
-        load(xb_sb[1][:], planes(xb, 2, 4))
         load(xa_sb[1][:], planes(xa, 2, 4))
         for q in range(4):
             load_scale_rows(w2_scales, R, q, nc.gpsimd)
@@ -90,8 +89,8 @@ def tile_list_sum_boundedgaps_largest_abovetable_residual_kernel(
         load(so_sb[:, 0:2, :].rearrange("p t c -> p (t c)"), planes(so, 0, 2))
         load(xo_sb[2], planes(xo, 2, 3))
         load(words_in[0][:].bitcast(I32), w_words[0].bitcast(I32))
-        load(fl_sb[:], by_partition(fl))
         load(xo_sb[3], planes(xo, 3, 4))
+        load(fl_sb[:], by_partition(fl))
         load(so_sb[:, 2:4, :].rearrange("p t c -> p (t c)"), planes(so, 2, 4))
         load(words_in[1][:].bitcast(I32), w2_words[0].bitcast(I32))
         load(list_t[:], offs4)
@@ -99,10 +98,10 @@ def tile_list_sum_boundedgaps_largest_abovetable_residual_kernel(
             load(tb_sb[t], planes(tb, t, t + 1))
         load(wb_codes[:].bitcast(I32), wb_words[0].rearrange("p n t -> p (n t)").bitcast(I32))
         load(rs_sb[:], rs.rearrange("(h p) c -> p h c", h=2))
-        for q in range(4):
-            load_scale_rows(wb_scales, 2 * R, q)
         with nc.allow_non_contiguous_dma(reason="one factor for each output row"):
             load(gm_sb[:], gm.rearrange("(h p) o -> p (h o)", h=2))
+        for q in range(4):
+            load_scale_rows(wb_scales, 2 * R, q)
 
         def woven(x):
             return x.rearrange("p (c i t) -> p c t i", i=RUN, t=PACK)
@@ -132,8 +131,8 @@ def tile_list_sum_boundedgaps_largest_abovetable_residual_kernel(
         gap = sb("gap", [P, PACK, J], F32)
         for t in range(PACK):
             cols = slice((t % 2) * S, (t % 2 + 1) * S)
-            gather(gb[:, t, :], xb_sb[t // 2][:, cols], list_b[:], False)
-            gather(ga[:, t, :], xa_sb[t // 2][:, cols], list_a[:], t < PACK - 1)
+            gather(gb[:, t, :], xb_sb[:, t * S : (t + 1) * S], list_b[:], t == 0)
+            gather(ga[:, t, :], xa_sb[t // 2][:, cols], list_a[:], t % 2 == 0)
             nc.vector.scalar_tensor_tensor(
                 gap[:, t, :], gb[:, t, :], hb_sb[:, t : t + 1], ga[:, t, :], ALU.min, ALU.subtract
             )
@@ -199,9 +198,14 @@ def tile_list_sum_boundedgaps_largest_abovetable_residual_kernel(
         gt = sb("gt", [P, PACK, J], F32)
         for t in range(2):
             gather(gt[:, t, :], tb_sb[t], list_t[:], False)
-        for t in range(2, PACK):
-            for h in range(2):
-                gather(gt[:, t, half_cols(h)], tb_sb[t], half_list(list_t, h), h == 0)
+        for h in range(2):
+            gather(gt[:, 2, half_cols(h)], tb_sb[2], half_list(list_t, h), h == 0)
+        for quarter in range(2):
+            gather(
+                gt[:, last, quarter * 64 : (quarter + 1) * 64], tb_sb[last],
+                list_t[:, quarter * 4 : (quarter + 1) * 4], quarter == 0,
+            )
+        gather(gt[:, last, half_cols(1)], tb_sb[last], half_list(list_t, 1), False)
 
         hid_bf = [sb(f"hid_bf{h}", [P, PACK * HALF], BF16) for h in range(2)]
         for h in range(2):

from contextlib import ExitStack

import concourse.mybir as mybir

K, T, J, S, R, F, Z, V, N = 512, 512, 256, 512, 512, 512, 1024, 512, 256
FLOPS = 2 * J * (K * R + F * R + R * N)

F32 = mybir.dt.float32
BF16 = mybir.dt.bfloat16
I32 = mybir.dt.int32
U32 = mybir.dt.uint32
U16 = mybir.dt.uint16
U8 = mybir.dt.uint8
E4M3 = mybir.dt.float8_e4m3fn_x4
E5M2 = mybir.dt.float8_e5m2_x4
E2M1 = mybir.dt.float4_e2m1fn_x4
ALU = mybir.AluOpType
COPY = mybir.ActivationFunctionType.Copy

P = 128
PACK = 4
HALF = J // 2
RUN = 4
LIST_COLS = J // 16


def tile_list_sum_boundedgaps_largest_abovetable_residual_kernel(
    tc, xa, xb, hb, fk, w_words, w_scales, xo, fl, so, w2_words, w2_scales, tb,
    wb_words, wb_scales, rs, gm, offs, offs2, offs3, offs4, out,
):
    nc = tc.nc
    with ExitStack() as ctx:
        pool = ctx.enter_context(tc.tile_pool(name="held", bufs=1))
        psum = ctx.enter_context(tc.psum_pool(name="psum", bufs=1))

        def sb(name, shape, dtype):
            return pool.tile(shape, dtype, name=name, align_bytes=64)

        list_a = sb("list_a", [P, LIST_COLS], U16)
        list_b = sb("list_b", [P, LIST_COLS], U16)
        list_o = sb("list_o", [P, LIST_COLS], U16)
        list_t = sb("list_t", [P, LIST_COLS], U16)
        xa_sb = [sb(f"xa{g}", [P, 2 * T], F32) for g in range(2)]
        xb_sb = sb("xb_sb", [P, PACK * S], F32)
        xo_pair = sb("xo_pair", [P, 2 * Z], F32)
        xo_sb = [xo_pair[:, 0:Z], xo_pair[:, Z : 2 * Z]] + [sb(f"xo{t}", [P, Z], F32)[:] for t in (2, 3)]
        tb_sb = [sb(f"tb{t}", [P, V], F32)[:] for t in range(PACK)]
        so_sb = sb("so_sb", [P, PACK, J], F32)
        rs_sb = sb("rs_sb", [P, 2, J], F32)
        hb_sb = sb("hb_sb", [P, PACK], F32)
        fk_sb = sb("fk_sb", [P, PACK], F32)
        fl_sb = sb("fl_sb", [P, PACK], F32)
        gm_sb = sb("gm_sb", [P, 2], F32)
        words_in = [sb(f"words_in{w}", [P, 2 * R], U8) for w in range(2)]
        scales_in = sb("scales_in", [P, 2 * R + N], U8)
        wb_codes = sb("wb_codes", [P, N], U32)

        def load(dst, src):
            nc.sync.dma_start(dst, src)

        def load_scale_rows(src, col0, q, queue=nc.sync):
            width = src.shape[2]
            queue.dma_start(
                scales_in[32 * q : 32 * q + 4, col0 : col0 + width].bitcast(I32),
                src[0, 4 * q : 4 * q + 4, :].bitcast(I32),
            )

        def by_partition(vec):
            return vec.rearrange("(p t) o -> p (t o)", t=PACK)

        nc.vector.memset(scales_in[:].bitcast(I32), 0)

        def planes(x, t0, t1):
            return x.rearrange("(p t) c -> p (t c)", t=PACK)[:, t0 * x.shape[1] : t1 * x.shape[1]]

        load(xb_sb[:], planes(xb, 0, 4))
        load(fk_sb[:], by_partition(fk))
        load(list_b[:], offs2)
        load(xa_sb[0][:], planes(xa, 0, 2))
        load(list_a[:], offs)
        load(hb_sb[:], by_partition(hb))
        load(xa_sb[1][:], planes(xa, 2, 4))
        for q in range(4):
            load_scale_rows(w2_scales, R, q, nc.gpsimd)
        load(list_o[:], offs3)
        load(xo_pair[:], planes(xo, 0, 2))
        for q in range(4):
            load_scale_rows(w_scales, 0, q)
        load(so_sb[:, 0:2, :].rearrange("p t c -> p (t c)"), planes(so, 0, 2))
        load(xo_sb[2], planes(xo, 2, 3))
        load(words_in[0][:].bitcast(I32), w_words[0].bitcast(I32))
        load(xo_sb[3], planes(xo, 3, 4))
        load(fl_sb[:], by_partition(fl))
        load(so_sb[:, 2:4, :].rearrange("p t c -> p (t c)"), planes(so, 2, 4))
        load(words_in[1][:].bitcast(I32), w2_words[0].bitcast(I32))
        load(list_t[:], offs4)
        for t in range(PACK):
            load(tb_sb[t], planes(tb, t, t + 1))
        load(wb_codes[:].bitcast(I32), wb_words[0].rearrange("p n t -> p (n t)").bitcast(I32))
        load(rs_sb[:], rs.rearrange("(h p) c -> p h c", h=2))
        with nc.allow_non_contiguous_dma(reason="one factor for each output row"):
            load(gm_sb[:], gm.rearrange("(h p) o -> p (h o)", h=2))
        for q in range(4):
            load_scale_rows(wb_scales, 2 * R, q)

        def woven(x):
            return x.rearrange("p (c i t) -> p c t i", i=RUN, t=PACK)

        def in_runs(x):
            return x.rearrange("p t (c i) -> p c t i", i=RUN)

        def spread(vec, width):
            return vec[:].unsqueeze(1).unsqueeze(3).to_broadcast([P, width // RUN, PACK, RUN])

        def half_cols(h):
            return slice(h * HALF, (h + 1) * HALF)

        def half_list(lst, h):
            return lst[:, h * LIST_COLS // 2 : (h + 1) * LIST_COLS // 2]

        def gather(dst, window, lst, on_vector):
            if on_vector:
                nc.vector.tensor_copy(dst, window.indirect(lst))
            else:
                nc.scalar.activation(dst, window.indirect(lst), COPY)

        fk_neg = sb("fk_neg", [P, PACK], F32)
        nc.scalar.activation(fk_neg[:], fk_sb[:], COPY, scale=-1.0)
        ga = sb("ga", [P, PACK, J], F32)
        gb = sb("gb", [P, PACK, J], F32)
        gap = sb("gap", [P, PACK, J], F32)
        for t in range(PACK):
            cols = slice((t % 2) * S, (t % 2 + 1) * S)
            gather(gb[:, t, :], xb_sb[:, t * S : (t + 1) * S], list_b[:], t == 0)
            gather(ga[:, t, :], xa_sb[t // 2][:, cols], list_a[:], t % 2 == 0)
            nc.vector.scalar_tensor_tensor(
                gap[:, t, :], gb[:, t, :], hb_sb[:, t : t + 1], ga[:, t, :], ALU.min, ALU.subtract
            )
        u_bf = sb("u_bf", [P, PACK * J], BF16)
        nc.vector.tensor_tensor(woven(u_bf[:]), in_runs(gap[:]), spread(fk_neg, J), ALU.mult)
        u_codes = sb("u_codes", [P, J], U32)
        u_scales = sb("u_scales", [P, J], U8)
        nc.vector.quantize_mx(u_codes[:].bitcast(E4M3), u_scales[:], u_bf[:])

        words = [sb(f"words{w}", [P, 2 * R], U8) for w in range(2)]
        scales = sb("scales", [P, 2 * R], U8)
        nc.vector.tensor_copy(
            scales[:].rearrange("p (w t m) -> p w t m", w=2, t=PACK),
            scales_in[:, 0 : 2 * R].rearrange("p (w m t) -> p w t m", w=2, t=PACK),
        )
        for w in range(2):
            nc.scalar.copy(
                words[w][:].bitcast(U16).rearrange("p (t m) -> p t m", t=PACK),
                words_in[w][:].bitcast(U16).rearrange("p (m t) -> p t m", t=PACK),
            )

        acc = [psum.tile([P, PACK, HALF], F32, name=f"acc{h}") for h in range(2)]

        def first_stage(h, w, codes, moving_scales):
            for t in range(PACK):
                col = t * P
                nc.tensor.matmul_mx(
                    acc[h][:, t, :],
                    lhsT=words[w][:, 2 * col : 2 * (col + P)].bitcast(E2M1),
                    lhsT_scale=scales[:, w * R + col : w * R + col + P],
                    rhs=codes.bitcast(E4M3),
                    rhs_scale=moving_scales,
                    start=(w == 0 and t == 0),
                    stop=(w == 1 and t == PACK - 1),
                )

        for h in range(2):
            first_stage(h, 0, u_codes[:, half_cols(h)], u_scales[:, half_cols(h)])

        go = sb("go", [P, PACK, J], F32)
        larger = sb("larger", [P, PACK, J], F32)
        for t in range(PACK - 1):
            nc.scalar.activation(go[:, t, :], xo_sb[t].indirect(list_o[:]), COPY)
        nc.vector.tensor_tensor(larger[:, 0:2, :], go[:, 0:2, :], so_sb[:, 0:2, :], ALU.max)
        last = PACK - 1
        nc.vector.tensor_copy(go[:, last, half_cols(0)], xo_sb[last].indirect(half_list(list_o, 0)))
        nc.scalar.activation(go[:, last, half_cols(1)], xo_sb[last].indirect(half_list(list_o, 1)), COPY)
        for h in range(2):
            nc.vector.tensor_tensor(
                larger[:, 2:4, half_cols(h)], go[:, 2:4, half_cols(h)], so_sb[:, 2:4, half_cols(h)], ALU.max
            )
        u2_bf = [sb(f"u2_bf{h}", [P, PACK * HALF], BF16) for h in range(2)]
        for h in range(2):
            nc.vector.tensor_tensor(
                woven(u2_bf[h][:]), in_runs(larger[:, :, half_cols(h)]), spread(fl_sb, HALF), ALU.mult
            )
        for h in range(2):
            u2_codes = sb(f"u2_codes{h}", [P, HALF], U32)
            u2_scales = sb(f"u2_scales{h}", [P, HALF], U8)
            nc.vector.quantize_mx(u2_codes[:].bitcast(E4M3), u2_scales[:], u2_bf[h][:])
            first_stage(h, 1, u2_codes[:], u2_scales[:])

        gt = sb("gt", [P, PACK, J], F32)
        for t in range(2):
            gather(gt[:, t, :], tb_sb[t], list_t[:], False)
        for h in range(2):
            gather(gt[:, 2, half_cols(h)], tb_sb[2], half_list(list_t, h), h == 0)
        for quarter in range(2):
            gather(
                gt[:, last, quarter * 64 : (quarter + 1) * 64], tb_sb[last],
                list_t[:, quarter * 4 : (quarter + 1) * 4], quarter == 0,
            )
        gather(gt[:, last, half_cols(1)], tb_sb[last], half_list(list_t, 1), False)

        hid_bf = [sb(f"hid_bf{h}", [P, PACK * HALF], BF16) for h in range(2)]
        for h in range(2):
            nc.vector.tensor_tensor(
                woven(hid_bf[h][:]), in_runs(acc[h][:]), in_runs(gt[:, :, half_cols(h)]), ALU.max
            )
        prod = [psum.tile([P, 2, HALF], F32, name=f"prod{h}") for h in range(2)]
        for h in range(2):
            hid_codes = sb(f"hid_codes{h}", [P, HALF], U32)
            hid_scales = sb(f"hid_scales{h}", [P, HALF], U8)
            nc.vector.quantize_mx(hid_codes[:].bitcast(E5M2), hid_scales[:], hid_bf[h][:])
            for g in range(2):
                nc.tensor.matmul_mx(
                    prod[h][:, g, :],
                    lhsT=wb_codes[:, g * P : (g + 1) * P].bitcast(E4M3),
                    lhsT_scale=scales_in[:, 2 * R + g * P : 2 * R + (g + 1) * P],
                    rhs=hid_codes[:].bitcast(E5M2),
                    rhs_scale=hid_scales[:],
                    start=True,
                    stop=True,
                )
        out_rows = out.rearrange("(g p) c -> p g c", g=2)
        for h in range(2):
            y = sb(f"y{h}", [P, 2, HALF], F32)
            for g in range(2):
                nc.vector.scalar_tensor_tensor(
                    y[:, g, :], prod[h][:, g, :], gm_sb[:, g : g + 1], rs_sb[:, g, half_cols(h)], ALU.mult, ALU.add
                )
                nc.sync.dma_start(out_rows[:, g, half_cols(h)], y[:, g, :])
